import numpy as np
import ml_dtypes


def mxq(x, axis, fmt="e4m3"):
    dtype, down = {"e4m3": (ml_dtypes.float8_e4m3fn, 7), "e5m2": (ml_dtypes.float8_e5m2, 14)}[fmt]
    v = np.moveaxis(np.asarray(x, np.float32).astype(ml_dtypes.bfloat16).astype(np.float64), axis, -1)
    blocks = v.reshape(v.shape[:-1] + (-1, 32))
    amax = np.abs(blocks).max(-1, keepdims=True)
    byte = np.maximum(np.where(amax > 0, np.frexp(amax)[1] - 1 + 127, 0) - down, 1)
    scale = np.exp2(byte - 127.0)
    codes = (blocks / scale).astype(np.float32).astype(dtype).astype(np.float64)
    return np.moveaxis((codes * scale).reshape(v.shape), -1, axis)


WIDE = False


def mx_kscale(k):
    if not WIDE:
        return np.ones(k)
    levels = np.array([30, -30])
    if k % 512:
        return np.exp2(np.random.permutation(np.resize(levels, k // 32))).repeat(32)
    a = np.empty((k // 512, 16))
    for p in range(k // 512):
        a[p, :8] = np.random.permutation(np.resize(levels, 8))
        for g in range(8):
            far = levels[np.abs(levels - a[p, g]) >= 10]
            a[p, g + 8] = far[np.random.randint(len(far))]
    return np.exp2(a.ravel()).repeat(32)


def f64(x):
    return np.asarray(x).astype(np.float64)


def striped(idx):
    return np.tile(np.asarray(idx).reshape(-1, 16).T, (8, 1)).astype(np.uint16)


def unstriped(offs):
    return offs[:16].T.reshape(-1).astype(np.int64)


E2M1 = np.array([0.0, 0.5, 1.0, 1.5, 2.0, 3.0, 4.0, 6.0, -0.0, -0.5, -1.0, -1.5, -2.0, -3.0, -4.0, -6.0])


def pack_weight(w, fmt):
    k, n = w.shape
    w = f64(np.asarray(w, np.float32).astype(ml_dtypes.bfloat16)).reshape(k // 32, 32, n)
    amax = np.abs(w).max(1)
    if fmt in ("e4m3", "e5m2"):
        byte = np.frexp(amax)[1] - 1 + 127 - (7 if fmt == "e4m3" else 14)
    else:
        mant, ex = np.frexp(amax / 6.0)
        byte = np.where(mant > 0.5, ex, ex - 1) + 127
    byte = np.clip(np.where(amax > 0, byte, 1), 1, 254)
    scaled = (w * np.exp2(127.0 - byte)[:, None, :]).reshape(k, n).astype(np.float32)
    by_word = np.ascontiguousarray(scaled.reshape(k // 512, 128, 4, n).transpose(0, 1, 3, 2))
    if fmt in ("e4m3", "e5m2"):
        words = by_word.astype(ml_dtypes.float8_e4m3fn if fmt == "e4m3" else ml_dtypes.float8_e5m2).view(np.uint8)
    else:
        c = by_word.astype(ml_dtypes.float4_e2m1fn).view(np.uint8) & 0xF
        words = (c[..., 0::2] | (c[..., 1::2] << 4)).reshape(k // 512, 128, 2 * n)
    return np.ascontiguousarray(words), np.ascontiguousarray(byte.astype(np.uint8).reshape(k // 512, 16, n))


def unpack_weight(words, scales, fmt):
    g, _, n = scales.shape
    words = np.ascontiguousarray(words).reshape(g, 128, n, -1)
    if fmt in ("e4m3", "e5m2"):
        vals = words.view(ml_dtypes.float8_e4m3fn if fmt == "e4m3" else ml_dtypes.float8_e5m2).astype(np.float64)
    else:
        nib = np.empty((g, 128, n, 4), np.uint8)
        nib[..., 0::2] = words & 0xF
        nib[..., 1::2] = words >> 4
        vals = E2M1[nib]
    vals = vals * np.repeat(np.exp2(scales.astype(np.float64) - 127.0), 8, axis=1)[..., None]
    return vals.transpose(0, 1, 3, 2).reshape(g * 512, n)


K, T, J, N, M = 1024, 1024, 256, 256, 128


def setup_inputs():
    n = np.random.standard_normal
    idx = np.random.permutation(T)[:J]
    idx2 = np.random.permutation(N)[:M]
    idx3 = np.random.permutation(N)[:M]
    fk = mx_kscale(K)
    xtp = pack_weight(n((K, T)) * np.random.uniform(0.4, 1.6, (1, T)) / fk[:, None], "e5m2")
    wap = pack_weight(n((K, N)) * 1 / np.sqrt(K) * fk[:, None], "e2m1")
    return {
        "xt_words": xtp[0],
        "xt_scales": xtp[1],
        "wa_words": wap[0],
        "wa_scales": wap[1],
        "wb": (n((K, N)) * 1 / np.sqrt(K) * fk[:, None]).astype(np.float32),
        "bi": (np.random.uniform(-0.6, 0.6, (1, N))).astype(np.float32),
        "cj": (np.random.uniform(0.5, 2.0, (J, 1))).astype(np.float32),
        "offs": striped(idx),
        "offs2": striped(idx2),
        "offs3": striped(idx3),
    }


def reference(xt_words, xt_scales, wa_words, wa_scales, wb, bi, cj, offs, offs2, offs3):
    idx = unstriped(offs)
    idx2 = unstriped(offs2)
    idx3 = unstriped(offs3)
    xtu = unpack_weight(xt_words, xt_scales, "e5m2")
    wau = unpack_weight(wa_words, wa_scales, "e2m1")
    xtidxg = xtu[:, idx]
    a = xtidxg.T @ wau
    wbq = mxq(f64(wb), 0, "e4m3")
    b0 = xtidxg.T @ wbq
    b2 = b0 + f64(bi)
    y = (a[:, idx2] - b2[:, idx3]) * f64(cj)
    return y

from contextlib import ExitStack

import concourse.mybir as mybir
from concourse.masks import make_identity

K, T, J, N, M = 1024, 1024, 256, 256, 128
FLOPS = 2 * 2 * K * J * N

F32 = mybir.dt.float32
BF16 = mybir.dt.bfloat16
I32 = mybir.dt.int32
U32 = mybir.dt.uint32
U16 = mybir.dt.uint16
U8 = mybir.dt.uint8
E4M3 = mybir.dt.float8_e4m3fn_x4
E5M2 = mybir.dt.float8_e5m2_x4
E2M1 = mybir.dt.float4_e2m1fn_x4
COPY = mybir.ActivationFunctionType.Copy
MULT = mybir.AluOpType.mult
ADD = mybir.AluOpType.add

P = 128
PACK = 4
PASSES = K // (P * PACK)
SLOT_TILES = J // P
QUADRANTS = 4
VECTOR_COLUMNS = 160


def interleaved(rounded, raw, columns):
    dst = rounded[:, columns, :].rearrange("p (c i) t -> p c t i", i=4)
    src = raw[:, :, columns].rearrange("p t (c i) -> p c t i", i=4)
    return dst, src


def tile_list_rows_onetoken_lookedtarget_kernel(tc, xt_words, xt_scales, wa_words, wa_scales, wb, bi, cj, offs, offs2, offs3, out):
    nc = tc.nc
    with ExitStack() as ctx:
        lists = ctx.enter_context(tc.tile_pool(name="lists", bufs=1))
        keep = ctx.enter_context(tc.tile_pool(name="keep", bufs=1))
        psum = ctx.enter_context(tc.psum_pool(name="psum", bufs=1))

        token_list = lists.tile([P, J // 16], U16)
        a_list = lists.tile([P, M // 16], U16)
        b_list = lists.tile([P, M // 16], U16)
        nc.sync.dma_start(token_list[:], offs)
        nc.sync.dma_start(a_list[:], offs2)
        nc.sync.dma_start(b_list[:], offs3)

        xt_scale_table = keep.tile([P, PASSES, T], U8, align_bytes=64)
        wa_scale = keep.tile([P, PASSES, N], U8, align_bytes=64)
        nc.gpsimd.memset(xt_scale_table[:].bitcast(I32), 0)

        xt_word_table = []
        wb_raw = []
        for z in range(PASSES):
            table = keep.tile([P, T], I32, name=f"xt_word_table{z}", align_bytes=64)
            nc.sync.dma_start(table[:], xt_words[z].rearrange("p c r -> p (c r)").bitcast(I32))
            xt_word_table.append(table)
            raw = keep.tile([P, PACK, N], F32, name=f"wb_raw{z}", align_bytes=64)
            nc.sync.dma_start(raw[:], wb[z * P * PACK:(z + 1) * P * PACK, :].rearrange("(p t) n -> p t n", t=PACK))
            wb_raw.append(raw)

        wa_codes = keep.tile([P, PASSES, 2 * N], U8, align_bytes=64)
        nc.scalar.dma_start(wa_codes[:].bitcast(I32), wa_words.rearrange("z p c -> p z c").bitcast(I32))
        for q, queue in enumerate((nc.scalar, nc.scalar, nc.gpsimd, nc.gpsimd)):
            queue.dma_start(
                wa_scale[32 * q:32 * q + 4, :, :].bitcast(I32),
                wa_scales[:, 4 * q:4 * q + 4, :].rearrange("z r c -> r z c").bitcast(I32),
            )
        for q in range(QUADRANTS):
            nc.scalar.dma_start(
                xt_scale_table[32 * q:32 * q + 4, :, :].bitcast(I32),
                xt_scales[:, 4 * q:4 * q + 4, :].rearrange("z r c -> r z c").bitcast(I32),
            )
        bias_pairs = keep.tile([P, 2], F32)
        nc.gpsimd.dma_start(bias_pairs[:], bi.rearrange("o (p e) -> (o p) e", e=2))
        identity = keep.tile([P, P], F32)
        make_identity(nc, identity[:])
        factor = keep.tile([P, SLOT_TILES], F32)
        with nc.allow_non_contiguous_dma(reason="one factor a partition"):
            nc.gpsimd.dma_start(factor[:], cj.rearrange("(s p) o -> p (s o)", p=P))
        bias_bank = psum.tile([P, 2, P], F32)
        for e in range(2):
            nc.tensor.transpose(bias_bank[:, e, :], bias_pairs[:, e:e + 1].to_broadcast([P, P]), identity[:])
        bias = keep.tile([P, N], F32)
        nc.scalar.copy(bias[:].rearrange("p (n e) -> p n e", e=2), bias_bank[:].rearrange("p e n -> p n e"))

        x_scale = []
        x_codes = []
        for z in range(PASSES):
            words = keep.tile([P, J], U32, name=f"x_codes{z}", align_bytes=64)
            nc.vector.tensor_copy(words[:], xt_word_table[z][:].bitcast(U32).indirect(token_list[:]))
            x_codes.append(words)
            scale = keep.tile([P, J], U8, name=f"x_scale{z}", align_bytes=64)
            nc.vector.tensor_copy(scale[:], xt_scale_table[:, z, :].indirect(token_list[:]))
            x_scale.append(scale)

        def multiply(bank, s, z, codes, scale):
            slots = slice(s * P, (s + 1) * P)
            nc.tensor.matmul_mx(
                out=bank[:], lhsT=x_codes[z][:, slots].bitcast(E5M2), lhsT_scale=x_scale[z][:, slots],
                rhs=codes, rhs_scale=scale, start=(z == 0), stop=(z == PASSES - 1),
            )

        a_banks = [psum.tile([P, N], F32, name=f"a_bank{s}") for s in range(SLOT_TILES)]
        b_banks = [psum.tile([P, N], F32, name=f"b_bank{s}") for s in range(SLOT_TILES)]
        for z in range(PASSES):
            for s in range(SLOT_TILES):
                multiply(a_banks[s], s, z, wa_codes[:, z, :].bitcast(E2M1), wa_scale[:, z, :])

        for z in range(PASSES):
            rounded = keep.tile([P, N, PACK], BF16, name=f"wb_rounded{z}", align_bytes=64)
            if z < PASSES - 1:
                nc.scalar.copy(*interleaved(rounded, wb_raw[z], slice(0, N)))
            else:
                nc.vector.tensor_copy(*interleaved(rounded, wb_raw[z], slice(0, VECTOR_COLUMNS)))
                nc.scalar.copy(*interleaved(rounded, wb_raw[z], slice(VECTOR_COLUMNS, N)))
            wb_codes = keep.tile([P, N], U32, name=f"wb_codes{z}", align_bytes=64)
            wb_scale = keep.tile([P, N], U8, name=f"wb_scale{z}", align_bytes=64)
            nc.vector.quantize_mx(out=wb_codes[:].bitcast(E4M3), scales=wb_scale[:], in_=rounded[:].rearrange("p n t -> p (n t)"))
            for s in range(SLOT_TILES):
                multiply(b_banks[s], s, z, wb_codes[:].bitcast(E4M3), wb_scale[:])

        a_terms = []
        for s in range(SLOT_TILES):
            a = keep.tile([P, N], F32, name=f"a{s}")
            nc.scalar.copy(a[:], a_banks[s][:])
            a_picked = keep.tile([P, M], F32, name=f"a_picked{s}")
            nc.scalar.activation(a_picked[:], a[:].indirect(a_list[:]), COPY)
            a_term = keep.tile([P, M], F32, name=f"a_term{s}")
            nc.vector.tensor_scalar(a_term[:], a_picked[:], factor[:, s:s + 1], None, MULT)
            a_terms.append(a_term)

        b_picks = []
        for s in range(SLOT_TILES):
            b2 = keep.tile([P, N], F32, name=f"b2_{s}")
            nc.vector.tensor_tensor(b2[:], b_banks[s][:], bias[:], ADD)
            b_picked = keep.tile([P, M], F32, name=f"b_picked{s}")
            nc.scalar.activation(b_picked[:], b2[:].indirect(b_list[:]), COPY, scale=-1.0)
            b_picks.append(b_picked)
        for s in range(SLOT_TILES):
            result = keep.tile([P, M], F32, name=f"result{s}")
            nc.vector.scalar_tensor_tensor(result[:], b_picks[s][:], factor[:, s:s + 1], a_terms[s][:], MULT, ADD)
            nc.sync.dma_start(out[s * P:(s + 1) * P, :], result[:])
